import numpy as np
import ml_dtypes


def mxq(x, axis, fmt="e4m3"):
    dtype, down = {"e4m3": (ml_dtypes.float8_e4m3fn, 7), "e5m2": (ml_dtypes.float8_e5m2, 14)}[fmt]
    v = np.moveaxis(np.asarray(x, np.float32).astype(ml_dtypes.bfloat16).astype(np.float64), axis, -1)
    blocks = v.reshape(v.shape[:-1] + (-1, 32))
    amax = np.abs(blocks).max(-1, keepdims=True)
    byte = np.maximum(np.where(amax > 0, np.frexp(amax)[1] - 1 + 127, 0) - down, 1)
    scale = np.exp2(byte - 127.0)
    codes = (blocks / scale).astype(np.float32).astype(dtype).astype(np.float64)
    return np.moveaxis((codes * scale).reshape(v.shape), -1, axis)


WIDE = False


def mx_kscale(k):
    if not WIDE:
        return np.ones(k)
    levels = np.array([30, -30])
    if k % 512:
        return np.exp2(np.random.permutation(np.resize(levels, k // 32))).repeat(32)
    a = np.empty((k // 512, 16))
    for p in range(k // 512):
        a[p, :8] = np.random.permutation(np.resize(levels, 8))
        for g in range(8):
            far = levels[np.abs(levels - a[p, g]) >= 10]
            a[p, g + 8] = far[np.random.randint(len(far))]
    return np.exp2(a.ravel()).repeat(32)


def f64(x):
    return np.asarray(x).astype(np.float64)


def striped(idx):
    return np.tile(np.asarray(idx).reshape(-1, 16).T, (8, 1)).astype(np.uint16)


def unstriped(offs):
    return offs[:16].T.reshape(-1).astype(np.int64)


E2M1 = np.array([0.0, 0.5, 1.0, 1.5, 2.0, 3.0, 4.0, 6.0, -0.0, -0.5, -1.0, -1.5, -2.0, -3.0, -4.0, -6.0])


def pack_weight(w, fmt):
    k, n = w.shape
    w = f64(np.asarray(w, np.float32).astype(ml_dtypes.bfloat16)).reshape(k // 32, 32, n)
    amax = np.abs(w).max(1)
    if fmt == "e4m3":
        byte = np.frexp(amax)[1] - 1 + 127 - 7
    else:
        mant, ex = np.frexp(amax / 6.0)
        byte = np.where(mant > 0.5, ex, ex - 1) + 127
    byte = np.clip(np.where(amax > 0, byte, 1), 1, 254)
    scaled = (w * np.exp2(127.0 - byte)[:, None, :]).reshape(k, n).astype(np.float32)
    by_word = np.ascontiguousarray(scaled.reshape(k // 512, 128, 4, n).transpose(0, 1, 3, 2))
    if fmt == "e4m3":
        words = by_word.astype(ml_dtypes.float8_e4m3fn).view(np.uint8)
    else:
        c = by_word.astype(ml_dtypes.float4_e2m1fn).view(np.uint8) & 0xF
        words = (c[..., 0::2] | (c[..., 1::2] << 4)).reshape(k // 512, 128, 2 * n)
    return np.ascontiguousarray(words), np.ascontiguousarray(byte.astype(np.uint8).reshape(k // 512, 16, n))


def unpack_weight(words, scales, fmt):
    g, _, n = scales.shape
    words = np.ascontiguousarray(words).reshape(g, 128, n, -1)
    if fmt == "e4m3":
        vals = words.view(ml_dtypes.float8_e4m3fn).astype(np.float64)
    else:
        nib = np.empty((g, 128, n, 4), np.uint8)
        nib[..., 0::2] = words & 0xF
        nib[..., 1::2] = words >> 4
        vals = E2M1[nib]
    vals = vals * np.repeat(np.exp2(scales.astype(np.float64) - 127.0), 8, axis=1)[..., None]
    return vals.transpose(0, 1, 3, 2).reshape(g * 512, n)


K, T, J, R, C, O, N, U = 512, 1024, 256, 512, 512, 256, 256, 128


def setup_inputs():
    n = np.random.standard_normal
    idx = np.random.permutation(T)[:J]
    idx2 = np.random.permutation(C)[:J]
    idx3 = np.random.permutation(C)[:O]
    idx4 = np.random.permutation(C)[:O]
    idx5 = np.random.permutation(T)[:O]
    idx6 = np.random.permutation(O)[:U]
    idx7 = np.random.permutation(O)[:U]
    fk = mx_kscale(K)
    fr = mx_kscale(R)
    xtp = pack_weight(n((K, T)) / fk[:, None], "e2m1")
    wp = pack_weight(n((K, R)) * 1 / np.sqrt(K) * fk[:, None] * fr, "e4m3")
    wbp = pack_weight(n((R, N)) * 1 / np.sqrt(R) / fr[:, None], "e2m1")
    wsp = pack_weight(n((K, N)) * 1 / np.sqrt(K) * fk[:, None], "e4m3")
    return {
        "xt_words": xtp[0],
        "xt_scales": xtp[1],
        "w_words": wp[0],
        "w_scales": wp[1],
        "sa": (np.random.uniform(0.5, 1.6, (R, 1))).astype(np.float32),
        "sb": (np.random.uniform(0.5, 1.6, (R, 1))).astype(np.float32),
        "wb_words": wbp[0],
        "wb_scales": wbp[1],
        "ws_words": wsp[0],
        "ws_scales": wsp[1],
        "so": (np.random.uniform(0.5, 1.6, (N, 1))).astype(np.float32),
        "offs": striped(idx),
        "offs2": striped(idx2),
        "offs3": striped(idx3),
        "offs4": striped(idx4),
        "offs5": striped(idx5),
        "offs6": striped(idx6),
        "offs7": striped(idx7),
    }


def reference(xt_words, xt_scales, w_words, w_scales, sa, sb, wb_words, wb_scales, ws_words, ws_scales, so, offs, offs2, offs3, offs4, offs5, offs6, offs7):
    idx = unstriped(offs)
    idx2 = unstriped(offs2)
    idx3 = unstriped(offs3)
    idx4 = unstriped(offs4)
    idx5 = unstriped(offs5)
    idx6 = unstriped(offs6)
    idx7 = unstriped(offs7)
    xtu = unpack_weight(xt_words, xt_scales, "e2m1")
    wu = unpack_weight(w_words, w_scales, "e4m3")
    wbu = unpack_weight(wb_words, wb_scales, "e2m1")
    wsu = unpack_weight(ws_words, ws_scales, "e4m3")
    xtidxg = xtu[:, idx]
    a = wu.T @ xtidxg
    pw = np.zeros((R, C))
    pw[:, idx2] = a
    hid = np.abs(pw[:, idx3] * f64(sa) - pw[:, idx4] * f64(sb))
    hidq = mxq(hid, 0, "e5m2")
    xtidx5g = xtu[:, idx5]
    p = wbu.T @ hidq + wsu.T @ xtidx5g
    y = p[:, idx6] - p[:, idx7] * f64(so)
    return y

@@ -1,0 +1,219 @@
+from contextlib import ExitStack
+
+import concourse.mybir as mybir
+
+K, T, J, R, C, O, N, U = 512, 1024, 256, 512, 512, 256, 256, 128
+FLOPS = 2 * K * R * J + 2 * R * N * O + 2 * K * N * O
+
+F32 = mybir.dt.float32
+BF16 = mybir.dt.bfloat16
+I32 = mybir.dt.int32
+U32 = mybir.dt.uint32
+U16 = mybir.dt.uint16
+U8 = mybir.dt.uint8
+E4M3X4 = mybir.dt.float8_e4m3fn_x4
+E5M2X4 = mybir.dt.float8_e5m2_x4
+E2M1X4 = mybir.dt.float4_e2m1fn_x4
+ACT = mybir.ActivationFunctionType
+ALU = mybir.AluOpType
+
+P = 128
+PACK = 4
+HALF = O // 2
+
+
+def tile_list_boardtwiceweighed_solo_further_weighedout_kernel(
+    tc, xt_words, xt_scales, w_words, w_scales, sa, sb, wb_words, wb_scales, ws_words, ws_scales, so,
+    offs, offs2, offs3, offs4, offs5, offs6, offs7, out,
+):
+    nc = tc.nc
+    with ExitStack() as ctx:
+        keep = ctx.enter_context(tc.tile_pool(name="keep", bufs=1))
+        psum = ctx.enter_context(tc.psum_pool(name="psum", bufs=1))
+
+        def sbuf(name, shape, dtype):
+            return keep.tile(shape, dtype, name=name, align_bytes=64)
+
+        def load_list(name, source):
+            tile = sbuf(name, list(source.shape), U16)
+            nc.sync.dma_start(tile[:], source)
+            return tile
+
+        def zeroed_plane(name, columns):
+            plane = sbuf(name, [P, columns], U8)
+            nc.vector.memset(plane[:].bitcast(I32), 0)
+            return plane
+
+        def load_scale_rows(plane, scales):
+            for q in range(4):
+                nc.sync.dma_start(
+                    plane[32 * q : 32 * q + 4, :].bitcast(I32), scales[0, 4 * q : 4 * q + 4, :].bitcast(I32)
+                )
+
+        xt_plane = zeroed_plane("xt_plane", T)
+        w_plane = sbuf("w_plane", [P, 4, R], U8)
+        nc.vector.memset(w_plane[:, 0, :].bitcast(I32), 0)
+        ws_plane = zeroed_plane("ws_plane", N)
+        wb_plane = zeroed_plane("wb_plane", N)
+        boards = [sbuf(f"board{t}", [P, C], F32) for t in range(PACK)]
+        for board in boards:
+            nc.vector.memset(board[:], 0.0)
+
+        xt_codes = sbuf("xt_codes", [P, T], U16)
+        w_codes = sbuf("w_codes", [P, R], U32)
+        nc.sync.dma_start(xt_codes[:].bitcast(I32), xt_words[0].bitcast(I32))
+        list1 = load_list("list1", offs)
+        load_scale_rows(xt_plane, xt_scales)
+        nc.sync.dma_start(
+            w_plane[0:4, :, :].bitcast(I32), w_scales[0].rearrange("(q r) c -> r q c", r=4).bitcast(I32)
+        )
+        nc.sync.dma_start(w_codes[:].bitcast(I32), w_words[0].rearrange("p c r -> p (c r)").bitcast(I32))
+        list5 = load_list("list5", offs5)
+        list2 = load_list("list2", offs2)
+        sa_sb = sbuf("sa_sb", [P, PACK], F32)
+        sb_sb = sbuf("sb_sb", [P, PACK], F32)
+        nc.sync.dma_start(sa_sb[:], sa.rearrange("(p t) o -> p (t o)", t=PACK))
+        list3 = load_list("list3", offs3)
+        nc.sync.dma_start(sb_sb[:], sb.rearrange("(p t) o -> p (t o)", t=PACK))
+        list4 = load_list("list4", offs4)
+        ws_codes = sbuf("ws_codes", [P, N], U32)
+        wb_codes = sbuf("wb_codes", [P, 2 * N], U8)
+        nc.sync.dma_start(ws_codes[:].bitcast(I32), ws_words[0].rearrange("p c r -> p (c r)").bitcast(I32))
+        load_scale_rows(ws_plane, ws_scales)
+        nc.sync.dma_start(wb_codes[:].bitcast(I32), wb_words[0].bitcast(I32))
+        load_scale_rows(wb_plane, wb_scales)
+        so_sb = [sbuf(f"so_sb{h}", [P, 1], F32) for h in range(2)]
+        for h in range(2):
+            nc.sync.dma_start(so_sb[h][:], so[P * h : P * (h + 1), :])
+        list7 = load_list("list7", offs7)
+        list6 = load_list("list6", offs6)
+
+        x1_scales = sbuf("x1_scales", [P, J], U8)
+        x1_codes = sbuf("x1_codes", [P, J], U16)
+        nc.vector.tensor_copy(x1_codes[:], xt_codes[:].indirect(list1[:]))
+        nc.vector.tensor_copy(x1_scales[:], xt_plane[:].indirect(list1[:]))
+        for q in range(1, 4):
+            nc.vector.tensor_copy(w_plane[32 * q : 32 * q + 4, 0, :].bitcast(I32), w_plane[0:4, q, :].bitcast(I32))
+        wd_plane = sbuf("wd_plane", [P, R], U8)
+        nc.vector.tensor_copy(
+            wd_plane[:].rearrange("p (t m) -> p t m", t=PACK), w_plane[:, 0, :].rearrange("p (m t) -> p t m", t=PACK)
+        )
+
+        wd_codes = sbuf("wd_codes", [P, R], U32)
+        nc.vector.tensor_copy(
+            wd_codes[:].bitcast(I32).rearrange("p (t c i) -> p c t i", t=PACK, i=4),
+            w_codes[:].bitcast(I32).rearrange("p (c i t) -> p c t i", t=PACK, i=4),
+        )
+
+        x5_scales = sbuf("x5_scales", [P, O], U8)
+        x5_codes = sbuf("x5_codes", [P, O], U16)
+        nc.vector.tensor_copy(x5_scales[:], xt_plane[:].indirect(list5[:]))
+        nc.vector.tensor_copy(x5_codes[:], xt_codes[:].indirect(list5[:]))
+
+        a_ps23 = psum.tile([P, 2, J], F32, name="a_ps23")
+        a_ps = [psum.tile([P, J], F32, name=f"a_ps{t}")[:] for t in range(2)] + [a_ps23[:, 0, :], a_ps23[:, 1, :]]
+        for t in (2, 3, 0, 1):
+            cols = slice(P * t, P * (t + 1))
+            nc.tensor.matmul_mx(
+                a_ps[t], lhsT=wd_codes[:, cols].bitcast(E4M3X4), lhsT_scale=wd_plane[:, cols],
+                rhs=x1_codes[:].bitcast(E2M1X4), rhs_scale=x1_scales[:], start=True, stop=True,
+            )
+        a_sb = sbuf("a_sb", [P, PACK, J], F32)
+        nc.scalar.activation(a_sb[:, 2:4, :], a_ps23[:], ACT.Copy)
+        nc.vector.tensor_copy(a_sb[:, 0, :], a_ps[0])
+        nc.scalar.activation(a_sb[:, 1, :], a_ps[1], ACT.Copy)
+        for t in range(PACK - 1):
+            nc.vector.tensor_copy(boards[t][:].indirect(list2[:]), a_sb[:, t, :])
+        nc.scalar.activation(boards[3][:].indirect(list2[:]), a_sb[:, 3, :], ACT.Copy)
+
+        first = [sbuf(f"first{t}", [P, O], F32) for t in range(PACK)]
+        second = [sbuf(f"second{t}", [P, O], F32) for t in range(PACK)]
+        diff = sbuf("diff", [P, 2, PACK, HALF], F32)
+
+        def read_board(t, lo, hi):
+            entries = slice(lo // 16, hi // 16)
+            nc.scalar.activation(
+                first[t][:, lo:hi], boards[t][:].indirect(list3[:, entries]), ACT.Copy, scale=sa_sb[:, t : t + 1]
+            )
+            nc.scalar.activation(
+                second[t][:, lo:hi], boards[t][:].indirect(list4[:, entries]), ACT.Copy, scale=sb_sb[:, t : t + 1]
+            )
+
+        def subtract(t, g):
+            cols = slice(HALF * g, HALF * (g + 1))
+            nc.vector.tensor_tensor(diff[:, g, t, :], first[t][:, cols], second[t][:, cols], ALU.subtract)
+
+        def subtract_whole(t):
+            nc.vector.tensor_tensor(
+                diff[:, :, t, :], first[t][:].rearrange("p (g o) -> p g o", g=2),
+                second[t][:].rearrange("p (g o) -> p g o", g=2), ALU.subtract,
+            )
+
+        hid = [sbuf(f"hid{g}", [P, HALF, PACK], BF16) for g in range(2)]
+        hid_codes = [sbuf(f"hid_codes{g}", [P, HALF], U32) for g in range(2)]
+        hid_plane = [sbuf(f"hid_plane{g}", [P, HALF], U8) for g in range(2)]
+
+        def quantise(g):
+            nc.vector.quantize_mx(
+                out=hid_codes[g][:].bitcast(E5M2X4), scales=hid_plane[g][:],
+                in_=hid[g][:].rearrange("p o t -> p (o t)"),
+            )
+
+        for t in (0, 3):
+            read_board(t, 0, O)
+        for g in range(2):
+            for t in (1, 2):
+                read_board(t, HALF * g, HALF * (g + 1))
+        subtract_whole(0)
+        subtract(3, 0)
+        subtract(1, 0)
+        subtract(2, 0)
+        subtract(3, 1)
+        d0 = diff[:, 0, :, :].rearrange("p t o -> p o t")
+        nc.vector.scalar_tensor_tensor(hid[0][:], d0, -1.0, d0, ALU.mult, ALU.max)
+        subtract(1, 1)
+        subtract(2, 1)
+        quantise(0)
+        d1 = diff[:, 1, :, :].rearrange("p t o -> p o t")
+        nc.scalar.activation(hid[1][:, : HALF // 2, :], d1[:, : HALF // 2, :], ACT.Abs)
+        nc.vector.scalar_tensor_tensor(
+            hid[1][:, HALF // 2 :, :], d1[:, HALF // 2 :, :], -1.0, d1[:, HALF // 2 :, :], ALU.mult, ALU.max
+        )
+        quantise(1)
+
+        p_sb = [sbuf(f"p_sb{h}", [P, O], F32) for h in range(2)]
+        p_ps = {}
+        for g in range(2):
+            for h in range(2):
+                p_ps[g, h] = psum.tile([P, HALF], F32, name=f"p_ps{g}{h}")
+                rows = slice(P * h, P * (h + 1))
+                cols = slice(HALF * g, HALF * (g + 1))
+                nc.tensor.matmul_mx(
+                    p_ps[g, h][:], lhsT=ws_codes[:, rows].bitcast(E4M3X4), lhsT_scale=ws_plane[:, rows],
+                    rhs=x5_codes[:, cols].bitcast(E2M1X4), rhs_scale=x5_scales[:, cols], start=True, stop=False,
+                )
+        for g in range(2):
+            cols = slice(HALF * g, HALF * (g + 1))
+            for h in range(2):
+                rows = slice(P * h, P * (h + 1))
+                nc.tensor.matmul_mx(
+                    p_ps[g, h][:], lhsT=wb_codes[:, 2 * P * h : 2 * P * (h + 1)].bitcast(E2M1X4),
+                    lhsT_scale=wb_plane[:, rows],
+                    rhs=hid_codes[g][:].bitcast(E5M2X4), rhs_scale=hid_plane[g][:], start=False, stop=True,
+                )
+            nc.scalar.activation(p_sb[0][:, cols], p_ps[g, 0][:], ACT.Copy)
+            if g == 0:
+                nc.scalar.activation(p_sb[1][:, cols], p_ps[g, 1][:], ACT.Copy)
+            else:
+                nc.vector.tensor_copy(p_sb[1][:, cols], p_ps[g, 1][:])
+
+        taken = [sbuf(f"taken{h}", [P, U], F32) for h in range(2)]
+        y = [sbuf(f"y{h}", [P, U], F32) for h in range(2)]
+        for h in range(2):
+            nc.scalar.activation(taken[h][:], p_sb[h][:].indirect(list7[:]), ACT.Copy, scale=so_sb[h][:])
+        kept = sbuf("kept", [P, U], F32)
+        nc.vector.tensor_copy(kept[:], p_sb[1][:].indirect(list6[:]))
+        nc.vector.tensor_tensor(y[0][:], p_sb[0][:].indirect(list6[:]), taken[0][:], ALU.subtract)
+        nc.vector.tensor_tensor(y[1][:], kept[:], taken[1][:], ALU.subtract)
+        for h in range(2):
+            nc.sync.dma_start(out[P * h : P * (h + 1), :], y[h][:])

@@ -20,6 +20,7 @@ ALU = mybir.AluOpType
 P = 128
 PACK = 4
 HALF = O // 2
+SPLIT = 80
 
 
 def tile_list_boardtwiceweighed_solo_further_weighedout_kernel(
@@ -51,8 +52,7 @@ def tile_list_boardtwiceweighed_solo_further_weighedout_kernel(
                 )
 
         xt_plane = zeroed_plane("xt_plane", T)
-        w_plane = sbuf("w_plane", [P, 4, R], U8)
-        nc.vector.memset(w_plane[:, 0, :].bitcast(I32), 0)
+        w_plane = zeroed_plane("w_plane", R)
         ws_plane = zeroed_plane("ws_plane", N)
         wb_plane = zeroed_plane("wb_plane", N)
         boards = [sbuf(f"board{t}", [P, C], F32) for t in range(PACK)]
@@ -61,12 +61,11 @@ def tile_list_boardtwiceweighed_solo_further_weighedout_kernel(
 
         xt_codes = sbuf("xt_codes", [P, T], U16)
         w_codes = sbuf("w_codes", [P, R], U32)
-        nc.sync.dma_start(xt_codes[:].bitcast(I32), xt_words[0].bitcast(I32))
+        w_rows = sbuf("w_rows", [4, 4, R // 4], I32)
+        nc.sync.dma_start(w_rows[:], w_scales[0].rearrange("(q r) c -> r q c", r=4).bitcast(I32))
+        nc.scalar.dma_start(xt_codes[:].bitcast(I32), xt_words[0].bitcast(I32))
         list1 = load_list("list1", offs)
         load_scale_rows(xt_plane, xt_scales)
-        nc.sync.dma_start(
-            w_plane[0:4, :, :].bitcast(I32), w_scales[0].rearrange("(q r) c -> r q c", r=4).bitcast(I32)
-        )
         nc.sync.dma_start(w_codes[:].bitcast(I32), w_words[0].rearrange("p c r -> p (c r)").bitcast(I32))
         list5 = load_list("list5", offs5)
         list2 = load_list("list2", offs2)
@@ -88,21 +87,21 @@ def tile_list_boardtwiceweighed_solo_further_weighedout_kernel(
         list7 = load_list("list7", offs7)
         list6 = load_list("list6", offs6)
 
+        for q in range(4):
+            nc.vector.tensor_copy(w_plane[32 * q : 32 * q + 4, :].bitcast(I32), w_rows[:, q, :])
+        wd_plane = sbuf("wd_plane", [P, R], U8)
+        nc.vector.tensor_copy(
+            wd_plane[:].rearrange("p (t m) -> p t m", t=PACK), w_plane[:].rearrange("p (m t) -> p t m", t=PACK)
+        )
         x1_scales = sbuf("x1_scales", [P, J], U8)
         x1_codes = sbuf("x1_codes", [P, J], U16)
         nc.vector.tensor_copy(x1_codes[:], xt_codes[:].indirect(list1[:]))
         nc.vector.tensor_copy(x1_scales[:], xt_plane[:].indirect(list1[:]))
-        for q in range(1, 4):
-            nc.vector.tensor_copy(w_plane[32 * q : 32 * q + 4, 0, :].bitcast(I32), w_plane[0:4, q, :].bitcast(I32))
-        wd_plane = sbuf("wd_plane", [P, R], U8)
-        nc.vector.tensor_copy(
-            wd_plane[:].rearrange("p (t m) -> p t m", t=PACK), w_plane[:, 0, :].rearrange("p (m t) -> p t m", t=PACK)
-        )
 
         wd_codes = sbuf("wd_codes", [P, R], U32)
-        nc.vector.tensor_copy(
-            wd_codes[:].bitcast(I32).rearrange("p (t c i) -> p c t i", t=PACK, i=4),
-            w_codes[:].bitcast(I32).rearrange("p (c i t) -> p c t i", t=PACK, i=4),
+        nc.scalar.copy(
+            wd_codes[:].rearrange("p (t c i) -> p c t i", t=PACK, i=4),
+            w_codes[:].rearrange("p (c i t) -> p c t i", t=PACK, i=4),
         )
 
         x5_scales = sbuf("x5_scales", [P, O], U8)
@@ -110,24 +109,26 @@ def tile_list_boardtwiceweighed_solo_further_weighedout_kernel(
         nc.vector.tensor_copy(x5_scales[:], xt_plane[:].indirect(list5[:]))
         nc.vector.tensor_copy(x5_codes[:], xt_codes[:].indirect(list5[:]))
 
-        a_ps23 = psum.tile([P, 2, J], F32, name="a_ps23")
-        a_ps = [psum.tile([P, J], F32, name=f"a_ps{t}")[:] for t in range(2)] + [a_ps23[:, 0, :], a_ps23[:, 1, :]]
-        for t in (2, 3, 0, 1):
+        a_ps = [psum.tile([P, J], F32, name=f"a_ps{t}") for t in range(PACK)]
+        for t in range(PACK):
             cols = slice(P * t, P * (t + 1))
             nc.tensor.matmul_mx(
-                a_ps[t], lhsT=wd_codes[:, cols].bitcast(E4M3X4), lhsT_scale=wd_plane[:, cols],
+                a_ps[t][:], lhsT=wd_codes[:, cols].bitcast(E4M3X4), lhsT_scale=wd_plane[:, cols],
                 rhs=x1_codes[:].bitcast(E2M1X4), rhs_scale=x1_scales[:], start=True, stop=True,
             )
-        a_sb = sbuf("a_sb", [P, PACK, J], F32)
-        nc.scalar.activation(a_sb[:, 2:4, :], a_ps23[:], ACT.Copy)
-        nc.vector.tensor_copy(a_sb[:, 0, :], a_ps[0])
-        nc.scalar.activation(a_sb[:, 1, :], a_ps[1], ACT.Copy)
-        for t in range(PACK - 1):
-            nc.vector.tensor_copy(boards[t][:].indirect(list2[:]), a_sb[:, t, :])
-        nc.scalar.activation(boards[3][:].indirect(list2[:]), a_sb[:, 3, :], ACT.Copy)
+        read = [sbuf(f"read{t}", [P, 2 * O], F32) for t in range(PACK)]
+        first = [read[t][:, :O] for t in range(PACK)]
+        second = [read[t][:, O:] for t in range(PACK)]
+        a_sb = [read[1][:, HALF : HALF + J]] + [sbuf(f"a_sb{t}", [P, J], F32)[:] for t in range(1, PACK)]
+        for t in range(PACK):
+            if t % 2 == 0:
+                nc.scalar.activation(a_sb[t], a_ps[t][:], ACT.Copy)
+            else:
+                nc.vector.tensor_copy(a_sb[t], a_ps[t][:])
+        nc.scalar.activation(boards[0][:].indirect(list2[:]), a_sb[0], ACT.Copy)
+        for t in range(1, PACK):
+            nc.vector.tensor_copy(boards[t][:].indirect(list2[:]), a_sb[t])
 
-        first = [sbuf(f"first{t}", [P, O], F32) for t in range(PACK)]
-        second = [sbuf(f"second{t}", [P, O], F32) for t in range(PACK)]
         diff = sbuf("diff", [P, 2, PACK, HALF], F32)
 
         def read_board(t, lo, hi):
@@ -145,49 +146,47 @@ def tile_list_boardtwiceweighed_solo_further_weighedout_kernel(
 
         def subtract_whole(t):
             nc.vector.tensor_tensor(
-                diff[:, :, t, :], first[t][:].rearrange("p (g o) -> p g o", g=2),
-                second[t][:].rearrange("p (g o) -> p g o", g=2), ALU.subtract,
+                diff[:, :, t, :], first[t].rearrange("p (g o) -> p g o", g=2),
+                second[t].rearrange("p (g o) -> p g o", g=2), ALU.subtract,
             )
 
         hid = [sbuf(f"hid{g}", [P, HALF, PACK], BF16) for g in range(2)]
         hid_codes = [sbuf(f"hid_codes{g}", [P, HALF], U32) for g in range(2)]
         hid_plane = [sbuf(f"hid_plane{g}", [P, HALF], U8) for g in range(2)]
 
-        def quantise(g):
+        def magnitude(g):
+            nc.scalar.activation(
+                hid[g][:, :SPLIT, :].rearrange("p (c i) t -> p c t i", i=4),
+                diff[:, g, :, :SPLIT].rearrange("p t (c i) -> p c t i", i=4), ACT.Abs,
+            )
+            rest = diff[:, g, :, SPLIT:].rearrange("p t o -> p o t")
+            nc.vector.scalar_tensor_tensor(hid[g][:, SPLIT:, :], rest, -1.0, rest, ALU.mult, ALU.max)
+
+        for t in range(PACK - 1):
+            read_board(t, 0, O)
+        for g in range(2):
+            read_board(3, HALF * g, HALF * (g + 1))
+        subtract_whole(0)
+        subtract_whole(1)
+        subtract(2, 0)
+        subtract(3, 0)
+        subtract(2, 1)
+        magnitude(0)
+        subtract(3, 1)
+        magnitude(1)
+        for g in range(2):
             nc.vector.quantize_mx(
                 out=hid_codes[g][:].bitcast(E5M2X4), scales=hid_plane[g][:],
                 in_=hid[g][:].rearrange("p o t -> p (o t)"),
             )
 
-        for t in (0, 3):
-            read_board(t, 0, O)
-        for g in range(2):
-            for t in (1, 2):
-                read_board(t, HALF * g, HALF * (g + 1))
-        subtract_whole(0)
-        subtract(3, 0)
-        subtract(1, 0)
-        subtract(2, 0)
-        subtract(3, 1)
-        d0 = diff[:, 0, :, :].rearrange("p t o -> p o t")
-        nc.vector.scalar_tensor_tensor(hid[0][:], d0, -1.0, d0, ALU.mult, ALU.max)
-        subtract(1, 1)
-        subtract(2, 1)
-        quantise(0)
-        d1 = diff[:, 1, :, :].rearrange("p t o -> p o t")
-        nc.scalar.activation(hid[1][:, : HALF // 2, :], d1[:, : HALF // 2, :], ACT.Abs)
-        nc.vector.scalar_tensor_tensor(
-            hid[1][:, HALF // 2 :, :], d1[:, HALF // 2 :, :], -1.0, d1[:, HALF // 2 :, :], ALU.mult, ALU.max
-        )
-        quantise(1)
-
         p_sb = [sbuf(f"p_sb{h}", [P, O], F32) for h in range(2)]
         p_ps = {}
         for g in range(2):
+            cols = slice(HALF * g, HALF * (g + 1))
             for h in range(2):
                 p_ps[g, h] = psum.tile([P, HALF], F32, name=f"p_ps{g}{h}")
                 rows = slice(P * h, P * (h + 1))
-                cols = slice(HALF * g, HALF * (g + 1))
                 nc.tensor.matmul_mx(
                     p_ps[g, h][:], lhsT=ws_codes[:, rows].bitcast(E4M3X4), lhsT_scale=ws_plane[:, rows],
                     rhs=x5_codes[:, cols].bitcast(E2M1X4), rhs_scale=x5_scales[:, cols], start=True, stop=False,
@@ -195,10 +194,9 @@ def tile_list_boardtwiceweighed_solo_further_weighedout_kernel(
         for g in range(2):
             cols = slice(HALF * g, HALF * (g + 1))
             for h in range(2):
-                rows = slice(P * h, P * (h + 1))
                 nc.tensor.matmul_mx(
                     p_ps[g, h][:], lhsT=wb_codes[:, 2 * P * h : 2 * P * (h + 1)].bitcast(E2M1X4),
-                    lhsT_scale=wb_plane[:, rows],
+                    lhsT_scale=wb_plane[:, P * h : P * (h + 1)],
                     rhs=hid_codes[g][:].bitcast(E5M2X4), rhs_scale=hid_plane[g][:], start=False, stop=True,
                 )
             nc.scalar.activation(p_sb[0][:, cols], p_ps[g, 0][:], ACT.Copy)

from contextlib import ExitStack

import concourse.mybir as mybir

K, T, J, R, C, O, N, U = 512, 1024, 256, 512, 512, 256, 256, 128
FLOPS = 2 * K * R * J + 2 * R * N * O + 2 * K * N * O

F32 = mybir.dt.float32
BF16 = mybir.dt.bfloat16
I32 = mybir.dt.int32
U32 = mybir.dt.uint32
U16 = mybir.dt.uint16
U8 = mybir.dt.uint8
E4M3X4 = mybir.dt.float8_e4m3fn_x4
E5M2X4 = mybir.dt.float8_e5m2_x4
E2M1X4 = mybir.dt.float4_e2m1fn_x4
ACT = mybir.ActivationFunctionType
ALU = mybir.AluOpType

P = 128
PACK = 4
HALF = O // 2
SPLIT = 80


def tile_list_boardtwiceweighed_solo_further_weighedout_kernel(
    tc, xt_words, xt_scales, w_words, w_scales, sa, sb, wb_words, wb_scales, ws_words, ws_scales, so,
    offs, offs2, offs3, offs4, offs5, offs6, offs7, out,
):
    nc = tc.nc
    with ExitStack() as ctx:
        keep = ctx.enter_context(tc.tile_pool(name="keep", bufs=1))
        psum = ctx.enter_context(tc.psum_pool(name="psum", bufs=1))

        def sbuf(name, shape, dtype):
            return keep.tile(shape, dtype, name=name, align_bytes=64)

        def load_list(name, source):
            tile = sbuf(name, list(source.shape), U16)
            nc.sync.dma_start(tile[:], source)
            return tile

        def zeroed_plane(name, columns):
            plane = sbuf(name, [P, columns], U8)
            nc.vector.memset(plane[:].bitcast(I32), 0)
            return plane

        def load_scale_rows(plane, scales):
            for q in range(4):
                nc.sync.dma_start(
                    plane[32 * q : 32 * q + 4, :].bitcast(I32), scales[0, 4 * q : 4 * q + 4, :].bitcast(I32)
                )

        xt_plane = zeroed_plane("xt_plane", T)
        w_plane = zeroed_plane("w_plane", R)
        ws_plane = zeroed_plane("ws_plane", N)
        wb_plane = zeroed_plane("wb_plane", N)
        boards = [sbuf(f"board{t}", [P, C], F32) for t in range(PACK)]
        for board in boards:
            nc.vector.memset(board[:], 0.0)

        xt_codes = sbuf("xt_codes", [P, T], U16)
        w_codes = sbuf("w_codes", [P, R], U32)
        w_rows = sbuf("w_rows", [4, 4, R // 4], I32)
        nc.sync.dma_start(w_rows[:], w_scales[0].rearrange("(q r) c -> r q c", r=4).bitcast(I32))
        nc.scalar.dma_start(xt_codes[:].bitcast(I32), xt_words[0].bitcast(I32))
        list1 = load_list("list1", offs)
        load_scale_rows(xt_plane, xt_scales)
        nc.sync.dma_start(w_codes[:].bitcast(I32), w_words[0].rearrange("p c r -> p (c r)").bitcast(I32))
        list5 = load_list("list5", offs5)
        list2 = load_list("list2", offs2)
        sa_sb = sbuf("sa_sb", [P, PACK], F32)
        sb_sb = sbuf("sb_sb", [P, PACK], F32)
        nc.sync.dma_start(sa_sb[:], sa.rearrange("(p t) o -> p (t o)", t=PACK))
        list3 = load_list("list3", offs3)
        nc.sync.dma_start(sb_sb[:], sb.rearrange("(p t) o -> p (t o)", t=PACK))
        list4 = load_list("list4", offs4)
        ws_codes = sbuf("ws_codes", [P, N], U32)
        wb_codes = sbuf("wb_codes", [P, 2 * N], U8)
        nc.sync.dma_start(ws_codes[:].bitcast(I32), ws_words[0].rearrange("p c r -> p (c r)").bitcast(I32))
        load_scale_rows(ws_plane, ws_scales)
        nc.sync.dma_start(wb_codes[:].bitcast(I32), wb_words[0].bitcast(I32))
        load_scale_rows(wb_plane, wb_scales)
        so_sb = [sbuf(f"so_sb{h}", [P, 1], F32) for h in range(2)]
        for h in range(2):
            nc.sync.dma_start(so_sb[h][:], so[P * h : P * (h + 1), :])
        list7 = load_list("list7", offs7)
        list6 = load_list("list6", offs6)

        for q in range(4):
            nc.vector.tensor_copy(w_plane[32 * q : 32 * q + 4, :].bitcast(I32), w_rows[:, q, :])
        wd_plane = sbuf("wd_plane", [P, R], U8)
        nc.vector.tensor_copy(
            wd_plane[:].rearrange("p (t m) -> p t m", t=PACK), w_plane[:].rearrange("p (m t) -> p t m", t=PACK)
        )
        x1_scales = sbuf("x1_scales", [P, J], U8)
        x1_codes = sbuf("x1_codes", [P, J], U16)
        nc.vector.tensor_copy(x1_codes[:], xt_codes[:].indirect(list1[:]))
        nc.vector.tensor_copy(x1_scales[:], xt_plane[:].indirect(list1[:]))

        wd_codes = sbuf("wd_codes", [P, R], U32)
        nc.scalar.copy(
            wd_codes[:].rearrange("p (t c i) -> p c t i", t=PACK, i=4),
            w_codes[:].rearrange("p (c i t) -> p c t i", t=PACK, i=4),
        )

        x5_scales = sbuf("x5_scales", [P, O], U8)
        x5_codes = sbuf("x5_codes", [P, O], U16)
        nc.vector.tensor_copy(x5_scales[:], xt_plane[:].indirect(list5[:]))
        nc.vector.tensor_copy(x5_codes[:], xt_codes[:].indirect(list5[:]))

        a_ps = [psum.tile([P, J], F32, name=f"a_ps{t}") for t in range(PACK)]
        for t in range(PACK):
            cols = slice(P * t, P * (t + 1))
            nc.tensor.matmul_mx(
                a_ps[t][:], lhsT=wd_codes[:, cols].bitcast(E4M3X4), lhsT_scale=wd_plane[:, cols],
                rhs=x1_codes[:].bitcast(E2M1X4), rhs_scale=x1_scales[:], start=True, stop=True,
            )
        read = [sbuf(f"read{t}", [P, 2 * O], F32) for t in range(PACK)]
        first = [read[t][:, :O] for t in range(PACK)]
        second = [read[t][:, O:] for t in range(PACK)]
        a_sb = [read[1][:, HALF : HALF + J]] + [sbuf(f"a_sb{t}", [P, J], F32)[:] for t in range(1, PACK)]
        for t in range(PACK):
            if t % 2 == 0:
                nc.scalar.activation(a_sb[t], a_ps[t][:], ACT.Copy)
            else:
                nc.vector.tensor_copy(a_sb[t], a_ps[t][:])
        nc.scalar.activation(boards[0][:].indirect(list2[:]), a_sb[0], ACT.Copy)
        for t in range(1, PACK):
            nc.vector.tensor_copy(boards[t][:].indirect(list2[:]), a_sb[t])

        diff = sbuf("diff", [P, 2, PACK, HALF], F32)

        def read_board(t, lo, hi):
            entries = slice(lo // 16, hi // 16)
            nc.scalar.activation(
                first[t][:, lo:hi], boards[t][:].indirect(list3[:, entries]), ACT.Copy, scale=sa_sb[:, t : t + 1]
            )
            nc.scalar.activation(
                second[t][:, lo:hi], boards[t][:].indirect(list4[:, entries]), ACT.Copy, scale=sb_sb[:, t : t + 1]
            )

        def subtract(t, g):
            cols = slice(HALF * g, HALF * (g + 1))
            nc.vector.tensor_tensor(diff[:, g, t, :], first[t][:, cols], second[t][:, cols], ALU.subtract)

        def subtract_whole(t):
            nc.vector.tensor_tensor(
                diff[:, :, t, :], first[t].rearrange("p (g o) -> p g o", g=2),
                second[t].rearrange("p (g o) -> p g o", g=2), ALU.subtract,
            )

        hid = [sbuf(f"hid{g}", [P, HALF, PACK], BF16) for g in range(2)]
        hid_codes = [sbuf(f"hid_codes{g}", [P, HALF], U32) for g in range(2)]
        hid_plane = [sbuf(f"hid_plane{g}", [P, HALF], U8) for g in range(2)]

        def magnitude(g):
            nc.scalar.activation(
                hid[g][:, :SPLIT, :].rearrange("p (c i) t -> p c t i", i=4),
                diff[:, g, :, :SPLIT].rearrange("p t (c i) -> p c t i", i=4), ACT.Abs,
            )
            rest = diff[:, g, :, SPLIT:].rearrange("p t o -> p o t")
            nc.vector.scalar_tensor_tensor(hid[g][:, SPLIT:, :], rest, -1.0, rest, ALU.mult, ALU.max)

        for t in range(PACK - 1):
            read_board(t, 0, O)
        for g in range(2):
            read_board(3, HALF * g, HALF * (g + 1))
        subtract_whole(0)
        subtract_whole(1)
        subtract(2, 0)
        subtract(3, 0)
        subtract(2, 1)
        magnitude(0)
        subtract(3, 1)
        magnitude(1)
        for g in range(2):
            nc.vector.quantize_mx(
                out=hid_codes[g][:].bitcast(E5M2X4), scales=hid_plane[g][:],
                in_=hid[g][:].rearrange("p o t -> p (o t)"),
            )

        p_sb = [sbuf(f"p_sb{h}", [P, O], F32) for h in range(2)]
        p_ps = {}
        for g in range(2):
            cols = slice(HALF * g, HALF * (g + 1))
            for h in range(2):
                p_ps[g, h] = psum.tile([P, HALF], F32, name=f"p_ps{g}{h}")
                rows = slice(P * h, P * (h + 1))
                nc.tensor.matmul_mx(
                    p_ps[g, h][:], lhsT=ws_codes[:, rows].bitcast(E4M3X4), lhsT_scale=ws_plane[:, rows],
                    rhs=x5_codes[:, cols].bitcast(E2M1X4), rhs_scale=x5_scales[:, cols], start=True, stop=False,
                )
        for g in range(2):
            cols = slice(HALF * g, HALF * (g + 1))
            for h in range(2):
                nc.tensor.matmul_mx(
                    p_ps[g, h][:], lhsT=wb_codes[:, 2 * P * h : 2 * P * (h + 1)].bitcast(E2M1X4),
                    lhsT_scale=wb_plane[:, P * h : P * (h + 1)],
                    rhs=hid_codes[g][:].bitcast(E5M2X4), rhs_scale=hid_plane[g][:], start=False, stop=True,
                )
            nc.scalar.activation(p_sb[0][:, cols], p_ps[g, 0][:], ACT.Copy)
            if g == 0:
                nc.scalar.activation(p_sb[1][:, cols], p_ps[g, 1][:], ACT.Copy)
            else:
                nc.vector.tensor_copy(p_sb[1][:, cols], p_ps[g, 1][:])

        taken = [sbuf(f"taken{h}", [P, U], F32) for h in range(2)]
        y = [sbuf(f"y{h}", [P, U], F32) for h in range(2)]
        for h in range(2):
            nc.scalar.activation(taken[h][:], p_sb[h][:].indirect(list7[:]), ACT.Copy, scale=so_sb[h][:])
        kept = sbuf("kept", [P, U], F32)
        nc.vector.tensor_copy(kept[:], p_sb[1][:].indirect(list6[:]))
        nc.vector.tensor_tensor(y[0][:], p_sb[0][:].indirect(list6[:]), taken[0][:], ALU.subtract)
        nc.vector.tensor_tensor(y[1][:], kept[:], taken[1][:], ALU.subtract)
        for h in range(2):
            nc.sync.dma_start(out[P * h : P * (h + 1), :], y[h][:])
